import numpy as np
import ml_dtypes


def mxq(x, axis, fmt="e4m3"):
    dtype, down = {"e4m3": (ml_dtypes.float8_e4m3fn, 7), "e5m2": (ml_dtypes.float8_e5m2, 14)}[fmt]
    v = np.moveaxis(np.asarray(x, np.float32).astype(ml_dtypes.bfloat16).astype(np.float64), axis, -1)
    blocks = v.reshape(v.shape[:-1] + (-1, 32))
    amax = np.abs(blocks).max(-1, keepdims=True)
    byte = np.maximum(np.where(amax > 0, np.frexp(amax)[1] - 1 + 127, 0) - down, 1)
    scale = np.exp2(byte - 127.0)
    codes = (blocks / scale).astype(np.float32).astype(dtype).astype(np.float64)
    return np.moveaxis((codes * scale).reshape(v.shape), -1, axis)


WIDE = False


def mx_kscale(k):
    if not WIDE:
        return np.ones(k)
    levels = np.array([10, -10, 5, -5, 0])
    if k % 512:
        return np.exp2(np.random.permutation(np.resize(levels, k // 32))).repeat(32)
    a = np.empty((k // 512, 16))
    for p in range(k // 512):
        a[p, :8] = np.random.permutation(np.resize(levels, 8))
        for g in range(8):
            far = levels[np.abs(levels - a[p, g]) >= 10]
            a[p, g + 8] = far[np.random.randint(len(far))]
    return np.exp2(a.ravel()).repeat(32)


def f64(x):
    return np.asarray(x).astype(np.float64)


E2M1 = np.array([0.0, 0.5, 1.0, 1.5, 2.0, 3.0, 4.0, 6.0, -0.0, -0.5, -1.0, -1.5, -2.0, -3.0, -4.0, -6.0])


def pack_weight(w, fmt):
    k, n = w.shape
    w = f64(np.asarray(w, np.float32).astype(ml_dtypes.bfloat16)).reshape(k // 32, 32, n)
    amax = np.abs(w).max(1)
    if fmt == "e4m3":
        byte = np.frexp(amax)[1] - 1 + 127 - 7
    else:
        mant, ex = np.frexp(amax / 6.0)
        byte = np.where(mant > 0.5, ex, ex - 1) + 127
    byte = np.clip(np.where(amax > 0, byte, 1), 1, 254)
    scaled = (w * np.exp2(127.0 - byte)[:, None, :]).reshape(k, n).astype(np.float32)
    by_word = np.ascontiguousarray(scaled.reshape(k // 512, 128, 4, n).transpose(0, 1, 3, 2))
    if fmt == "e4m3":
        words = by_word.astype(ml_dtypes.float8_e4m3fn).view(np.uint8)
    else:
        c = by_word.astype(ml_dtypes.float4_e2m1fn).view(np.uint8) & 0xF
        words = (c[..., 0::2] | (c[..., 1::2] << 4)).reshape(k // 512, 128, 2 * n)
    return np.ascontiguousarray(words), np.ascontiguousarray(byte.astype(np.uint8).reshape(k // 512, 16, n))


def unpack_weight(words, scales, fmt):
    g, _, n = scales.shape
    words = np.ascontiguousarray(words).reshape(g, 128, n, -1)
    if fmt == "e4m3":
        vals = words.view(ml_dtypes.float8_e4m3fn).astype(np.float64)
    else:
        nib = np.empty((g, 128, n, 4), np.uint8)
        nib[..., 0::2] = words & 0xF
        nib[..., 1::2] = words >> 4
        vals = E2M1[nib]
    vals = vals * np.repeat(np.exp2(scales.astype(np.float64) - 127.0), 8, axis=1)[..., None]
    return vals.transpose(0, 1, 3, 2).reshape(g * 512, n)


K, M, T = 1536, 512, 512


def setup_inputs():
    n = np.random.standard_normal
    s = mx_kscale(K)[:, None]
    p_w4 = pack_weight(n((K, M)) / np.sqrt(K) / s ** 2, "e2m1")
    p_w8 = pack_weight(n((K, M)) / np.sqrt(K) / s, "e4m3")
    return {
        "x": (n((K, T)) * s).astype(np.float32),
        "w4_words": p_w4[0],
        "w4_scales": p_w4[1],
        "w8_words": p_w8[0],
        "w8_scales": p_w8[1],
        "r": (n((512, 512))).astype(np.float32),
    }


def reference(x, w4_words, w4_scales, w8_words, w8_scales, r):
    xa_, xb_ = mxq(f64(x) ** 2, 0, "e4m3"), mxq(f64(x), 0, "e4m3")
    w4_ = unpack_weight(w4_words, w4_scales, "e2m1")
    w8_ = unpack_weight(w8_words, w8_scales, "e4m3")
    y = w4_.T @ xa_ + w8_.T @ xb_
    return f64(r) + y

@@ -1,0 +1,162 @@
+from contextlib import ExitStack
+
+import concourse.mybir as mybir
+
+K, M, T = 1536, 512, 512
+FLOPS = 2 * 2 * K * M * T
+
+F32 = mybir.dt.float32
+BF16 = mybir.dt.bfloat16
+I32 = mybir.dt.int32
+U32 = mybir.dt.uint32
+U8 = mybir.dt.uint8
+FP8X4 = mybir.dt.float8_e4m3fn_x4
+FP4X4 = mybir.dt.float4_e2m1fn_x4
+
+P = 128
+PACK = 4
+K_PASS = P * PACK
+PASSES = K // K_PASS
+N_TILES = M // P
+HALVES = 2
+T_HALF = T // HALVES
+RUN = 4
+W8_ROW0 = 4
+
+
+def tile_mix_feat_fm_quad_res_kernel(tc, x, w4_words, w4_scales, w8_words, w8_scales, r, out):
+    nc = tc.nc
+    chunks = [(a, h) for a in range(PASSES) for h in range(HALVES)]
+
+    with ExitStack() as ctx:
+        sb = ctx.enter_context(tc.tile_pool(name="sb", bufs=1))
+        psum = ctx.enter_context(tc.psum_pool(name="psum", bufs=1))
+        ctx.enter_context(tc.manual_schedule())
+
+        x_raw = {c: sb.tile([P, PACK, T_HALF], F32, name="x_raw_%d_%d" % c, align_bytes=64) for c in chunks}
+        w4_sb = [sb.tile([P, 2 * M], U8, name="w4_%d" % a, align_bytes=64) for a in range(PASSES)]
+        w8_sb = [sb.tile([P, M], U32, name="w8_%d" % a, align_bytes=64) for a in range(PASSES)]
+        w4_plane = sb.tile([P, PASSES * M], U8, name="w4_plane", align_bytes=64)
+        w8_plane = sb.tile([P, PASSES * M], U8, name="w8_plane", align_bytes=64)
+        r_sb = [sb.tile([P, T], F32, name="r_%d" % i, align_bytes=64) for i in range(N_TILES)]
+        acc = {
+            (i, h): psum.tile([P, T_HALF], F32, name="acc_%d_%d" % (i, h))
+            for h in range(HALVES)
+            for i in range(N_TILES)
+        }
+
+        def load_x(c):
+            a, h = c
+            rows = x[a * K_PASS : (a + 1) * K_PASS, h * T_HALF : (h + 1) * T_HALF]
+            nc.sync.dma_start(out=x_raw[c][:], in_=rows.rearrange("(p j) t -> p j t", j=PACK))
+
+        def load_w4(a):
+            nc.sync.dma_start(out=w4_sb[a][:].bitcast(I32), in_=w4_words[a].bitcast(I32))
+
+        def load_w8(a):
+            nc.sync.dma_start(
+                out=w8_sb[a][:].bitcast(I32), in_=w8_words[a].rearrange("p n i -> p (n i)").bitcast(I32)
+            )
+
+        def load_scales(plane, scales, row0):
+            for s in range(4):
+                nc.sync.dma_start(
+                    out=plane[:].bitcast(I32)[row0 + s : P : 32, :].rearrange("q (a n) -> q a n", a=PASSES),
+                    in_=scales.bitcast(I32)[:, s:16:4, :].rearrange("a q n -> q a n"),
+                )
+
+        def load_r(i):
+            nc.sync.dma_start(out=r_sb[i][:], in_=r[i * P : (i + 1) * P, :])
+
+        nc.vector.memset(w8_plane[:].bitcast(I32), 0)
+        nc.vector.memset(w4_plane[:].bitcast(I32), 0)
+
+        load_x((0, 0))
+        load_x((0, 1))
+        load_scales(w8_plane, w8_scales, W8_ROW0)
+        load_w8(0)
+        load_x((1, 0))
+        load_scales(w4_plane, w4_scales, 0)
+        load_w4(0)
+        load_x((1, 1))
+        load_w8(1)
+        load_w4(1)
+        load_x((2, 0))
+        load_x((2, 1))
+        load_w8(2)
+        load_w4(2)
+        for i in range(N_TILES):
+            load_r(i)
+
+        def walk_raw(c):
+            return x_raw[c][:].rearrange("p j (b e) -> p b j e", e=RUN)
+
+        def walk_grouped(tile):
+            return tile[:].rearrange("p (b e j) -> p b j e", e=RUN, j=PACK)
+
+        def grouped_tile(name, c):
+            return sb.tile([P, T_HALF * PACK], BF16, name="%s_%d_%d" % (name, c[0], c[1]), align_bytes=64)
+
+        def quantize(name, c, grouped):
+            codes = sb.tile([P, T_HALF], U32, name="%s_codes_%d_%d" % (name, c[0], c[1]), align_bytes=64)
+            plane = sb.tile([P, T_HALF], U8, name="%s_plane_%d_%d" % (name, c[0], c[1]), align_bytes=64)
+            nc.vector.quantize_mx(out=codes[:].bitcast(FP8X4), scales=plane[:], in_=grouped[:])
+            return codes, plane
+
+        def multiply_w8(c, xb):
+            a, h = c
+            for i in range(N_TILES):
+                nc.tensor.matmul_mx(
+                    out=acc[i, h][:],
+                    lhsT=w8_sb[a][:, i * P : (i + 1) * P].bitcast(FP8X4),
+                    lhsT_scale=w8_plane[W8_ROW0:P, a * M + i * P : a * M + (i + 1) * P],
+                    rhs=xb[0][:].bitcast(FP8X4),
+                    rhs_scale=xb[1][:],
+                    start=(a == 0),
+                    stop=False,
+                )
+
+        def multiply_w4(c, xa):
+            a, h = c
+            for i in range(N_TILES):
+                nc.tensor.matmul_mx(
+                    out=acc[i, h][:],
+                    lhsT=w4_sb[a][:, 2 * i * P : 2 * (i + 1) * P].bitcast(FP4X4),
+                    lhsT_scale=w4_plane[:, a * M + i * P : a * M + (i + 1) * P],
+                    rhs=xa[0][:].bitcast(FP8X4),
+                    rhs_scale=xa[1][:],
+                    start=False,
+                    stop=(a == PASSES - 1),
+                )
+
+        squares = {}
+        xa = {}
+        xb = {}
+        for n, c in enumerate(chunks):
+            squares[c] = grouped_tile("xa", c)
+            nc.scalar.activation(
+                out=walk_grouped(squares[c]), in_=walk_raw(c), func=mybir.ActivationFunctionType.Square
+            )
+            linear = grouped_tile("xb", c)
+            nc.vector.tensor_copy(out=walk_grouped(linear), in_=walk_raw(c))
+            if n > 0:
+                xa[chunks[n - 1]] = quantize("xa", chunks[n - 1], squares[chunks[n - 1]])
+            xb[c] = quantize("xb", c, linear)
+        xa[chunks[-1]] = quantize("xa", chunks[-1], squares[chunks[-1]])
+
+        multiply_w8(chunks[0], xb[chunks[0]])
+        multiply_w8(chunks[1], xb[chunks[1]])
+        multiply_w4(chunks[0], xa[chunks[0]])
+        multiply_w4(chunks[1], xa[chunks[1]])
+        for c in chunks[2:]:
+            multiply_w8(c, xb[c])
+            multiply_w4(c, xa[c])
+
+        for h in range(HALVES):
+            cols = slice(h * T_HALF, (h + 1) * T_HALF)
+            for i in range(N_TILES):
+                result = sb.tile([P, T_HALF], F32, name="result_%d_%d" % (i, h), align_bytes=64)
+                nc.vector.tensor_tensor(
+                    out=result[:], in0=acc[i, h][:], in1=r_sb[i][:, cols], op=mybir.AluOpType.add
+                )
+                nc.sync.dma_start(out=out[i * P : (i + 1) * P, cols], in_=result[:])

@@ -33,8 +33,16 @@ def tile_mix_feat_fm_quad_res_kernel(tc, x, w4_words, w4_scales, w8_words, w8_sc
         psum = ctx.enter_context(tc.psum_pool(name="psum", bufs=1))
         ctx.enter_context(tc.manual_schedule())
 
-        x_raw = {c: sb.tile([P, PACK, T_HALF], F32, name="x_raw_%d_%d" % c, align_bytes=64) for c in chunks}
-        w4_sb = [sb.tile([P, 2 * M], U8, name="w4_%d" % a, align_bytes=64) for a in range(PASSES)]
+        last = PASSES - 1
+        x_whole = [sb.tile([P, PACK, T], F32, name="x_whole_%d" % a, align_bytes=64) for a in range(last)]
+        x_last = [sb.tile([P, PACK, T_HALF], F32, name="x_last_%d" % h, align_bytes=64) for h in range(HALVES)]
+        x_raw = {
+            (a, h): x_last[h][:] if a == last else x_whole[a][:, :, h * T_HALF : (h + 1) * T_HALF]
+            for a, h in chunks
+        }
+        w4_early = sb.tile([P, last, 2 * M], U8, name="w4_early", align_bytes=64)
+        w4_last = sb.tile([P, 2 * M], U8, name="w4_last", align_bytes=64)
+        w4_sb = [w4_early[:, a, :] for a in range(last)] + [w4_last[:]]
         w8_sb = [sb.tile([P, M], U32, name="w8_%d" % a, align_bytes=64) for a in range(PASSES)]
         w4_plane = sb.tile([P, PASSES * M], U8, name="w4_plane", align_bytes=64)
         w8_plane = sb.tile([P, PASSES * M], U8, name="w8_plane", align_bytes=64)
@@ -45,13 +53,9 @@ def tile_mix_feat_fm_quad_res_kernel(tc, x, w4_words, w4_scales, w8_words, w8_sc
             for i in range(N_TILES)
         }
 
-        def load_x(c):
-            a, h = c
-            rows = x[a * K_PASS : (a + 1) * K_PASS, h * T_HALF : (h + 1) * T_HALF]
-            nc.sync.dma_start(out=x_raw[c][:], in_=rows.rearrange("(p j) t -> p j t", j=PACK))
-
-        def load_w4(a):
-            nc.sync.dma_start(out=w4_sb[a][:].bitcast(I32), in_=w4_words[a].bitcast(I32))
+        def load_x(tile, a, cols):
+            rows = x[a * K_PASS : (a + 1) * K_PASS, cols]
+            nc.sync.dma_start(out=tile[:], in_=rows.rearrange("(p j) t -> p j t", j=PACK))
 
         def load_w8(a):
             nc.sync.dma_start(
@@ -65,31 +69,27 @@ def tile_mix_feat_fm_quad_res_kernel(tc, x, w4_words, w4_scales, w8_words, w8_sc
                     in_=scales.bitcast(I32)[:, s:16:4, :].rearrange("a q n -> q a n"),
                 )
 
-        def load_r(i):
-            nc.sync.dma_start(out=r_sb[i][:], in_=r[i * P : (i + 1) * P, :])
-
         nc.vector.memset(w8_plane[:].bitcast(I32), 0)
         nc.vector.memset(w4_plane[:].bitcast(I32), 0)
 
-        load_x((0, 0))
-        load_x((0, 1))
+        load_x(x_whole[0], 0, slice(0, T))
         load_scales(w8_plane, w8_scales, W8_ROW0)
         load_w8(0)
-        load_x((1, 0))
+        load_x(x_whole[1], 1, slice(0, T))
         load_scales(w4_plane, w4_scales, 0)
-        load_w4(0)
-        load_x((1, 1))
+        nc.sync.dma_start(
+            out=w4_early[:].bitcast(I32), in_=w4_words.bitcast(I32)[0:last].rearrange("a p n -> p a n")
+        )
         load_w8(1)
-        load_w4(1)
-        load_x((2, 0))
-        load_x((2, 1))
-        load_w8(2)
-        load_w4(2)
+        load_x(x_last[0], last, slice(0, T_HALF))
+        load_x(x_last[1], last, slice(T_HALF, T))
+        nc.sync.dma_start(out=w4_last[:].bitcast(I32), in_=w4_words.bitcast(I32)[last])
+        load_w8(last)
         for i in range(N_TILES):
-            load_r(i)
+            nc.sync.dma_start(out=r_sb[i][:], in_=r[i * P : (i + 1) * P, :])
 
         def walk_raw(c):
-            return x_raw[c][:].rearrange("p j (b e) -> p b j e", e=RUN)
+            return x_raw[c].rearrange("p j (b e) -> p b j e", e=RUN)
 
         def walk_grouped(tile):
             return tile[:].rearrange("p (b e j) -> p b j e", e=RUN, j=PACK)
@@ -103,9 +103,9 @@ def tile_mix_feat_fm_quad_res_kernel(tc, x, w4_words, w4_scales, w8_words, w8_sc
             nc.vector.quantize_mx(out=codes[:].bitcast(FP8X4), scales=plane[:], in_=grouped[:])
             return codes, plane
 
-        def multiply_w8(c, xb):
+        def multiply_w8(c, xb, tiles):
             a, h = c
-            for i in range(N_TILES):
+            for i in tiles:
                 nc.tensor.matmul_mx(
                     out=acc[i, h][:],
                     lhsT=w8_sb[a][:, i * P : (i + 1) * P].bitcast(FP8X4),
@@ -113,12 +113,12 @@ def tile_mix_feat_fm_quad_res_kernel(tc, x, w4_words, w4_scales, w8_words, w8_sc
                     rhs=xb[0][:].bitcast(FP8X4),
                     rhs_scale=xb[1][:],
                     start=(a == 0),
-                    stop=False,
+                    stop=(c == (last, 0)),
                 )
 
-        def multiply_w4(c, xa):
+        def multiply_w4(c, xa, tiles):
             a, h = c
-            for i in range(N_TILES):
+            for i in tiles:
                 nc.tensor.matmul_mx(
                     out=acc[i, h][:],
                     lhsT=w4_sb[a][:, 2 * i * P : 2 * (i + 1) * P].bitcast(FP4X4),
@@ -126,37 +126,56 @@ def tile_mix_feat_fm_quad_res_kernel(tc, x, w4_words, w4_scales, w8_words, w8_sc
                     rhs=xa[0][:].bitcast(FP8X4),
                     rhs_scale=xa[1][:],
                     start=False,
-                    stop=(a == PASSES - 1),
+                    stop=(c == (last, 1)),
                 )
 
         squares = {}
+        linear = {}
         xa = {}
         xb = {}
-        for n, c in enumerate(chunks):
+
+        def square(c):
             squares[c] = grouped_tile("xa", c)
             nc.scalar.activation(
                 out=walk_grouped(squares[c]), in_=walk_raw(c), func=mybir.ActivationFunctionType.Square
             )
-            linear = grouped_tile("xb", c)
-            nc.vector.tensor_copy(out=walk_grouped(linear), in_=walk_raw(c))
+
+        def cast(c):
+            linear[c] = grouped_tile("xb", c)
+            nc.vector.tensor_copy(out=walk_grouped(linear[c]), in_=walk_raw(c))
+
+        def quantize_xa(c):
+            xa[c] = quantize("xa", c, squares[c])
+
+        def quantize_xb(c):
+            xb[c] = quantize("xb", c, linear[c])
+
+        for c in chunks:
+            square(c)
+        for n, c in enumerate(chunks):
+            cast(c)
             if n > 0:
-                xa[chunks[n - 1]] = quantize("xa", chunks[n - 1], squares[chunks[n - 1]])
-            xb[c] = quantize("xb", c, linear)
-        xa[chunks[-1]] = quantize("xa", chunks[-1], squares[chunks[-1]])
+                quantize_xa(chunks[n - 1])
+            quantize_xb(c)
+        quantize_xa(chunks[-1])
 
-        multiply_w8(chunks[0], xb[chunks[0]])
-        multiply_w8(chunks[1], xb[chunks[1]])
-        multiply_w4(chunks[0], xa[chunks[0]])
-        multiply_w4(chunks[1], xa[chunks[1]])
-        for c in chunks[2:]:
-            multiply_w8(c, xb[c])
-            multiply_w4(c, xa[c])
+        every_tile = range(N_TILES)
+        for a in range(last):
+            for h in range(HALVES):
+                multiply_w8((a, h), xb[a, h], every_tile)
+            for h in range(HALVES):
+                multiply_w4((a, h), xa[a, h], every_tile)
+        multiply_w4((last, 0), xa[last, 0], every_tile)
+        for i in every_tile:
+            multiply_w8((last, 0), xb[last, 0], [i])
+            multiply_w8((last, 1), xb[last, 1], [i])
+            multiply_w4((last, 1), xa[last, 1], [i])
 
-        for h in range(HALVES):
-            cols = slice(h * T_HALF, (h + 1) * T_HALF)
-            for i in range(N_TILES):
-                result = sb.tile([P, T_HALF], F32, name="result_%d_%d" % (i, h), align_bytes=64)
+        for i in every_tile:
+            result = sb.tile([P, T], F32, name="result_%d" % i, align_bytes=64)
+            for h in range(HALVES):
+                cols = slice(h * T_HALF, (h + 1) * T_HALF)
                 nc.vector.tensor_tensor(
-                    out=result[:], in0=acc[i, h][:], in1=r_sb[i][:, cols], op=mybir.AluOpType.add
+                    out=result[:, cols], in0=acc[i, h][:], in1=r_sb[i][:, cols], op=mybir.AluOpType.add
                 )
-                nc.sync.dma_start(out=out[i * P : (i + 1) * P, cols], in_=result[:])
+            nc.sync.dma_start(out=out[i * P : (i + 1) * P, :], in_=result[:])

from contextlib import ExitStack

import concourse.mybir as mybir

K, M, T = 1536, 512, 512
FLOPS = 2 * 2 * K * M * T

F32 = mybir.dt.float32
BF16 = mybir.dt.bfloat16
I32 = mybir.dt.int32
U32 = mybir.dt.uint32
U8 = mybir.dt.uint8
FP8X4 = mybir.dt.float8_e4m3fn_x4
FP4X4 = mybir.dt.float4_e2m1fn_x4

P = 128
PACK = 4
K_PASS = P * PACK
PASSES = K // K_PASS
N_TILES = M // P
HALVES = 2
T_HALF = T // HALVES
RUN = 4
W8_ROW0 = 4


def tile_mix_feat_fm_quad_res_kernel(tc, x, w4_words, w4_scales, w8_words, w8_scales, r, out):
    nc = tc.nc
    chunks = [(a, h) for a in range(PASSES) for h in range(HALVES)]

    with ExitStack() as ctx:
        sb = ctx.enter_context(tc.tile_pool(name="sb", bufs=1))
        psum = ctx.enter_context(tc.psum_pool(name="psum", bufs=1))
        ctx.enter_context(tc.manual_schedule())

        last = PASSES - 1
        x_whole = [sb.tile([P, PACK, T], F32, name="x_whole_%d" % a, align_bytes=64) for a in range(last)]
        x_last = [sb.tile([P, PACK, T_HALF], F32, name="x_last_%d" % h, align_bytes=64) for h in range(HALVES)]
        x_raw = {
            (a, h): x_last[h][:] if a == last else x_whole[a][:, :, h * T_HALF : (h + 1) * T_HALF]
            for a, h in chunks
        }
        w4_early = sb.tile([P, last, 2 * M], U8, name="w4_early", align_bytes=64)
        w4_last = sb.tile([P, 2 * M], U8, name="w4_last", align_bytes=64)
        w4_sb = [w4_early[:, a, :] for a in range(last)] + [w4_last[:]]
        w8_sb = [sb.tile([P, M], U32, name="w8_%d" % a, align_bytes=64) for a in range(PASSES)]
        w4_plane = sb.tile([P, PASSES * M], U8, name="w4_plane", align_bytes=64)
        w8_plane = sb.tile([P, PASSES * M], U8, name="w8_plane", align_bytes=64)
        r_sb = [sb.tile([P, T], F32, name="r_%d" % i, align_bytes=64) for i in range(N_TILES)]
        acc = {
            (i, h): psum.tile([P, T_HALF], F32, name="acc_%d_%d" % (i, h))
            for h in range(HALVES)
            for i in range(N_TILES)
        }

        def load_x(tile, a, cols):
            rows = x[a * K_PASS : (a + 1) * K_PASS, cols]
            nc.sync.dma_start(out=tile[:], in_=rows.rearrange("(p j) t -> p j t", j=PACK))

        def load_w8(a):
            nc.sync.dma_start(
                out=w8_sb[a][:].bitcast(I32), in_=w8_words[a].rearrange("p n i -> p (n i)").bitcast(I32)
            )

        def load_scales(plane, scales, row0):
            for s in range(4):
                nc.sync.dma_start(
                    out=plane[:].bitcast(I32)[row0 + s : P : 32, :].rearrange("q (a n) -> q a n", a=PASSES),
                    in_=scales.bitcast(I32)[:, s:16:4, :].rearrange("a q n -> q a n"),
                )

        nc.vector.memset(w8_plane[:].bitcast(I32), 0)
        nc.vector.memset(w4_plane[:].bitcast(I32), 0)

        load_x(x_whole[0], 0, slice(0, T))
        load_scales(w8_plane, w8_scales, W8_ROW0)
        load_w8(0)
        load_x(x_whole[1], 1, slice(0, T))
        load_scales(w4_plane, w4_scales, 0)
        nc.sync.dma_start(
            out=w4_early[:].bitcast(I32), in_=w4_words.bitcast(I32)[0:last].rearrange("a p n -> p a n")
        )
        load_w8(1)
        load_x(x_last[0], last, slice(0, T_HALF))
        load_x(x_last[1], last, slice(T_HALF, T))
        nc.sync.dma_start(out=w4_last[:].bitcast(I32), in_=w4_words.bitcast(I32)[last])
        load_w8(last)
        for i in range(N_TILES):
            nc.sync.dma_start(out=r_sb[i][:], in_=r[i * P : (i + 1) * P, :])

        def walk_raw(c):
            return x_raw[c].rearrange("p j (b e) -> p b j e", e=RUN)

        def walk_grouped(tile):
            return tile[:].rearrange("p (b e j) -> p b j e", e=RUN, j=PACK)

        def grouped_tile(name, c):
            return sb.tile([P, T_HALF * PACK], BF16, name="%s_%d_%d" % (name, c[0], c[1]), align_bytes=64)

        def quantize(name, c, grouped):
            codes = sb.tile([P, T_HALF], U32, name="%s_codes_%d_%d" % (name, c[0], c[1]), align_bytes=64)
            plane = sb.tile([P, T_HALF], U8, name="%s_plane_%d_%d" % (name, c[0], c[1]), align_bytes=64)
            nc.vector.quantize_mx(out=codes[:].bitcast(FP8X4), scales=plane[:], in_=grouped[:])
            return codes, plane

        def multiply_w8(c, xb, tiles):
            a, h = c
            for i in tiles:
                nc.tensor.matmul_mx(
                    out=acc[i, h][:],
                    lhsT=w8_sb[a][:, i * P : (i + 1) * P].bitcast(FP8X4),
                    lhsT_scale=w8_plane[W8_ROW0:P, a * M + i * P : a * M + (i + 1) * P],
                    rhs=xb[0][:].bitcast(FP8X4),
                    rhs_scale=xb[1][:],
                    start=(a == 0),
                    stop=(c == (last, 0)),
                )

        def multiply_w4(c, xa, tiles):
            a, h = c
            for i in tiles:
                nc.tensor.matmul_mx(
                    out=acc[i, h][:],
                    lhsT=w4_sb[a][:, 2 * i * P : 2 * (i + 1) * P].bitcast(FP4X4),
                    lhsT_scale=w4_plane[:, a * M + i * P : a * M + (i + 1) * P],
                    rhs=xa[0][:].bitcast(FP8X4),
                    rhs_scale=xa[1][:],
                    start=False,
                    stop=(c == (last, 1)),
                )

        squares = {}
        linear = {}
        xa = {}
        xb = {}

        def square(c):
            squares[c] = grouped_tile("xa", c)
            nc.scalar.activation(
                out=walk_grouped(squares[c]), in_=walk_raw(c), func=mybir.ActivationFunctionType.Square
            )

        def cast(c):
            linear[c] = grouped_tile("xb", c)
            nc.vector.tensor_copy(out=walk_grouped(linear[c]), in_=walk_raw(c))

        def quantize_xa(c):
            xa[c] = quantize("xa", c, squares[c])

        def quantize_xb(c):
            xb[c] = quantize("xb", c, linear[c])

        for c in chunks:
            square(c)
        for n, c in enumerate(chunks):
            cast(c)
            if n > 0:
                quantize_xa(chunks[n - 1])
            quantize_xb(c)
        quantize_xa(chunks[-1])

        every_tile = range(N_TILES)
        for a in range(last):
            for h in range(HALVES):
                multiply_w8((a, h), xb[a, h], every_tile)
            for h in range(HALVES):
                multiply_w4((a, h), xa[a, h], every_tile)
        multiply_w4((last, 0), xa[last, 0], every_tile)
        for i in every_tile:
            multiply_w8((last, 0), xb[last, 0], [i])
            multiply_w8((last, 1), xb[last, 1], [i])
            multiply_w4((last, 1), xa[last, 1], [i])

        for i in every_tile:
            result = sb.tile([P, T], F32, name="result_%d" % i, align_bytes=64)
            for h in range(HALVES):
                cols = slice(h * T_HALF, (h + 1) * T_HALF)
                nc.vector.tensor_tensor(
                    out=result[:, cols], in0=acc[i, h][:], in1=r_sb[i][:, cols], op=mybir.AluOpType.add
                )
            nc.sync.dma_start(out=out[i * P : (i + 1) * P, :], in_=result[:])
